import numpy as np
import ml_dtypes


def mxq(x, axis, fmt="e4m3"):
    dtype, down = {"e4m3": (ml_dtypes.float8_e4m3fn, 7), "e5m2": (ml_dtypes.float8_e5m2, 14)}[fmt]
    v = np.moveaxis(np.asarray(x, np.float32).astype(ml_dtypes.bfloat16).astype(np.float64), axis, -1)
    blocks = v.reshape(v.shape[:-1] + (-1, 32))
    amax = np.abs(blocks).max(-1, keepdims=True)
    byte = np.maximum(np.where(amax > 0, np.frexp(amax)[1] - 1 + 127, 0) - down, 1)
    scale = np.exp2(byte - 127.0)
    codes = (blocks / scale).astype(np.float32).astype(dtype).astype(np.float64)
    return np.moveaxis((codes * scale).reshape(v.shape), -1, axis)


WIDE = False


def mx_kscale(k):
    if not WIDE:
        return np.ones(k)
    levels = np.array([10, -10, 5, -5, 0])
    if k % 512:
        return np.exp2(np.random.permutation(np.resize(levels, k // 32))).repeat(32)
    a = np.empty((k // 512, 16))
    for p in range(k // 512):
        a[p, :8] = np.random.permutation(np.resize(levels, 8))
        for g in range(8):
            far = levels[np.abs(levels - a[p, g]) >= 10]
            a[p, g + 8] = far[np.random.randint(len(far))]
    return np.exp2(a.ravel()).repeat(32)


def f64(x):
    return np.asarray(x).astype(np.float64)


def striped(idx):
    return np.tile(idx.reshape(-1, 16).T, (8, 1)).astype(np.uint16)


def unstriped(offs):
    return offs[:16].T.reshape(-1).astype(np.int64)


def pack_weight(w):
    k, n = w.shape
    w = f64(np.asarray(w, np.float32).astype(ml_dtypes.bfloat16)).reshape(k // 32, 32, n)
    amax = np.abs(w).max(1)
    byte = np.clip(np.where(amax > 0, np.frexp(amax)[1] - 1 + 127 - 7, 1), 1, 254)
    scaled = (w * np.exp2(127.0 - byte)[:, None, :]).reshape(k, n).astype(np.float32)
    words = np.ascontiguousarray(scaled.reshape(k // 512, 128, 4, n).transpose(0, 1, 3, 2)).astype(ml_dtypes.float8_e4m3fn).view(np.uint8)
    return words, np.ascontiguousarray(byte.astype(np.uint8).reshape(k // 512, 16, n))


def unpack_weight(words, scales):
    g, p, n, _ = words.shape
    vals = np.ascontiguousarray(words).view(ml_dtypes.float8_e4m3fn).astype(np.float64) * np.repeat(np.exp2(scales.astype(np.float64) - 127.0), 8, axis=1)[..., None]
    return vals.transpose(0, 1, 3, 2).reshape(g * 512, n)


K, T, S, N, U = 1024, 1024, 512, 128, 512
P = 2 ** 7


def setup_inputs():
    n = np.random.standard_normal
    s = mx_kscale(K)[:, None]
    packed_xT = pack_weight(n((K, T)) * s)
    return {
        "x_words": packed_xT[0],
        "x_scales": packed_xT[1],
        "w1": (n((K, N)) / np.sqrt(K) / s).astype(np.float32),
        "leak": (np.tile(np.random.uniform(0.6, 1.2, U), (P, 1))).astype(np.float32),
        "cur": (np.random.uniform(0.0, 1.5, (N, U))).astype(np.float32),
        "deg": (np.random.uniform(0.2, 0.8, (N, 1))).astype(np.float32),
        "offs": striped(np.random.permutation(T)[:S]),
        "act1": striped(np.random.randint(0, S, U)),
        "act2": striped(np.random.randint(0, S, U)),
        "rep1": striped(np.random.randint(0, S, U)),
    }


def reference(x_words, x_scales, w1, leak, cur, deg, offs, act1, act2, rep1):
    xq = unpack_weight(x_words, x_scales)[:, unstriped(offs)]
    y = mxq(f64(w1), 0, "e4m3").T @ xq
    lev = np.log(np.exp(y) + 1.0)
    ga = lev[:, unstriped(act1)]
    pa = ((ga) ** 2) / ((ga) ** 2 + 0.5)
    gb = lev[:, unstriped(act2)]
    pb = ((gb) ** 2) / ((gb) ** 2 + 0.8)
    gr = lev[:, unstriped(rep1)]
    pr = f64(leak)[:1] / ((gr) ** 2 + 0.7)
    prd = (-1.0 * ((-1.0 * pa + 1.0) * (-1.0 * pb + 1.0)) + 1.0) * pr
    return 1.5 * prd - (f64(deg) * f64(cur))

@@ -1,0 +1,141 @@
+import math
+from contextlib import ExitStack
+
+import concourse.mybir as mybir
+
+K, T, S, M, U = 1024, 1024, 512, 128, 512
+FLOPS = 2 * K * M * S
+
+F32 = mybir.dt.float32
+BF16 = mybir.dt.bfloat16
+I32 = mybir.dt.int32
+U32 = mybir.dt.uint32
+U16 = mybir.dt.uint16
+U8 = mybir.dt.uint8
+FP8X4 = mybir.dt.float8_e4m3fn_x4
+ALU = mybir.AluOpType
+ACT = mybir.ActivationFunctionType
+
+P = 128
+PACK = 4
+K_PASS = P * PACK
+PASSES = K // K_PASS
+HALF = S // 2
+LIST_ROWS = 16
+FLOOR = 1e-18
+
+
+def tile_picked_ygrn_or_p_kernel(tc, x_words, x_scales, w1, leak, cur, deg, offs, act1, act2, rep1, out):
+    nc = tc.nc
+    halves = [slice(h * HALF, (h + 1) * HALF) for h in range(2)]
+    list_halves = [slice(h * HALF // LIST_ROWS, (h + 1) * HALF // LIST_ROWS) for h in range(2)]
+
+    with ExitStack() as ctx:
+        keep = ctx.enter_context(tc.tile_pool(name="keep", bufs=1))
+        psum = ctx.enter_context(tc.psum_pool(name="psum", bufs=1))
+
+        warm_in = keep.tile([P, 1], F32, name="warm_in")
+        warm_out = keep.tile([P, 1], F32, name="warm_out")
+        nc.gpsimd.memset(warm_in[:], 0.0)
+        nc.scalar.activation(out=warm_out[:], in_=warm_in[:], func=ACT.Sigmoid)
+
+        offs_sb = keep.tile([P, S // LIST_ROWS], U16, name="offs_sb")
+        nc.sync.dma_start(offs_sb[:], offs)
+
+        scales = keep.tile([P, T], U8, name="scales", align_bytes=64)
+        nc.vector.memset(scales[:].bitcast(I32), 0)
+        for q in range(4):
+            nc.sync.dma_start(out=scales[32 * q : 32 * q + 4 * PASSES, :].bitcast(I32), in_=x_scales[:, 4 * q : 4 * q + 4, :].bitcast(I32))
+
+        words = [keep.tile([P, T], I32, name="words%d" % g, align_bytes=64) for g in range(PASSES)]
+        w_raw = keep.tile([P, PASSES, PACK * M], F32, name="w_raw", align_bytes=64)
+        nc.sync.dma_start(out=words[0][:], in_=x_words[0].rearrange("p c t -> p (c t)").bitcast(I32))
+        nc.sync.dma_start(out=w_raw[:], in_=w1.rearrange("(g p j) m -> p g (j m)", g=PASSES, j=PACK))
+        nc.sync.dma_start(out=words[1][:], in_=x_words[1].rearrange("p c t -> p (c t)").bitcast(I32))
+
+        lists = []
+        for name, src in (("act1_sb", act1), ("act2_sb", act2), ("rep1_sb", rep1)):
+            tile_ = keep.tile([P, U // LIST_ROWS], U16, name=name)
+            nc.sync.dma_start(tile_[:], src)
+            lists.append(tile_)
+        act1_sb, act2_sb, rep1_sb = lists
+        leak_sb = keep.tile([P, U], F32, name="leak_sb")
+        cur_sb = keep.tile([P, U], F32, name="cur_sb")
+        deg_sb = keep.tile([P, 1], F32, name="deg_sb")
+        nc.sync.dma_start(out=deg_sb[:], in_=deg)
+        nc.sync.dma_start(out=leak_sb[:], in_=leak)
+        nc.sync.dma_start(out=cur_sb[:], in_=cur)
+        neg_deg = keep.tile([P, 1], F32, name="neg_deg")
+        nc.gpsimd.tensor_scalar(out=neg_deg[:], in0=deg_sb[:], scalar1=-1.0, scalar2=0.0, op0=ALU.mult, op1=ALU.add)
+
+        picked_scales = keep.tile([P, S], U8, name="picked_scales", align_bytes=64)
+        nc.vector.tensor_copy(picked_scales[:], scales[:].indirect(offs_sb[:]))
+        picked, w_codes, w_scales = [], [], []
+        for g in range(PASSES):
+            picked_g = keep.tile([P, S], U32, name="picked%d" % g, align_bytes=64)
+            if g == 0:
+                nc.vector.tensor_copy(picked_g[:], words[g][:].bitcast(U32).indirect(offs_sb[:]))
+            picked.append(picked_g)
+            grouped = keep.tile([P, M, PACK], BF16, name="grouped%d" % g, align_bytes=64)
+            nc.scalar.copy(out=grouped[:], in_=w_raw[:, g, :].rearrange("p (j m) -> p m j", j=PACK))
+            codes = keep.tile([P, M], U32, name="w_codes%d" % g, align_bytes=64)
+            plane = keep.tile([P, M], U8, name="w_scales%d" % g, align_bytes=64)
+            nc.vector.quantize_mx(out=codes[:].bitcast(FP8X4), scales=plane[:], in_=grouped[:].rearrange("p m j -> p (m j)"))
+            w_codes.append(codes)
+            w_scales.append(plane)
+
+        for h in range(2):
+            nc.vector.tensor_copy(picked[1][:, halves[h]], words[1][:].bitcast(U32).indirect(offs_sb[:, list_halves[h]]))
+        banks = [psum.tile([P, HALF], F32, name="y%d" % h) for h in range(2)]
+        for g in range(PASSES):
+            for h in range(2):
+                nc.tensor.matmul_mx(out=banks[h][:], lhsT=w_codes[g][:].bitcast(FP8X4), lhsT_scale=w_scales[g][:],
+                                    rhs=picked[g][:, halves[h]].bitcast(FP8X4), rhs_scale=picked_scales[4 * g :, halves[h]],
+                                    start=(g == 0), stop=(g == PASSES - 1))
+
+        sig = keep.tile([P, S], F32, name="sig")
+        y_floor = keep.tile([P, S], F32, name="y_floor")
+        for h in range(2):
+            nc.scalar.activation(out=sig[:, halves[h]], in_=banks[h][:], func=ACT.Sigmoid, scale=-1.0)
+        for h in range(2):
+            nc.vector.tensor_scalar(out=y_floor[:, halves[h]], in0=banks[h][:], scalar1=FLOOR, scalar2=None, op0=ALU.max)
+
+        neg_soft = keep.tile([P, S], F32, name="neg_soft")
+        lev = keep.tile([P, S], F32, name="lev")
+        log_lev = keep.tile([P, S], F32, name="log_lev")
+
+        def part(t, i):
+            return t[:].rearrange("p (h c) -> p h c", h=2)[:, :, i * (HALF // 2) : (i + 1) * (HALF // 2)]
+
+        for i in range(2):
+            nc.scalar.activation(out=part(neg_soft, i), in_=part(sig, i), func=ACT.Ln, bias=FLOOR)
+            nc.vector.scalar_tensor_tensor(out=part(lev, i), in0=part(neg_soft, i), scalar=-1.0, in1=part(y_floor, i), op0=ALU.mult, op1=ALU.max)
+        for i in range(2):
+            nc.scalar.activation(out=part(log_lev, i), in_=part(lev, i), func=ACT.Ln)
+
+        LEAD = 64
+        logs = keep.tile([P, 2 * U + LEAD], F32, name="logs")
+        ua = [logs[:, 0:HALF], logs[:, U + LEAD + HALF :]]
+        ub = [logs[:, HALF:U], logs[:, U + LEAD : U + LEAD + HALF]]
+        sr = logs[:, U : 2 * U]
+        sa = keep.tile([P, U], F32, name="sa")
+        sb = keep.tile([P, U], F32, name="sb")
+        both = keep.tile([P, U], F32, name="both")
+        either = keep.tile([P, U], F32, name="either")
+        prod = keep.tile([P, U], F32, name="prod")
+        res = keep.tile([P, U], F32, name="res")
+        for h in range(2):
+            nc.vector.tensor_copy(ua[h], log_lev[:].indirect(act1_sb[:, list_halves[h]]))
+            nc.vector.tensor_copy(ub[h], log_lev[:].indirect(act2_sb[:, list_halves[h]]))
+        for h in range(2):
+            nc.scalar.activation(out=sa[:, halves[h]], in_=ua[h], func=ACT.Sigmoid, scale=-2.0, bias=math.log(0.5))
+            nc.scalar.activation(out=sb[:, halves[h]], in_=ub[h], func=ACT.Sigmoid, scale=-2.0, bias=math.log(0.8))
+        for lo, hi in ((0, LEAD), (LEAD, HALF), (HALF, U)):
+            nc.scalar.activation(out=sr[:, lo:hi], in_=log_lev[:].indirect(rep1_sb[:, lo // LIST_ROWS : hi // LIST_ROWS]), func=ACT.Sigmoid, scale=-2.0, bias=math.log(0.7))
+        for h in range(2):
+            nc.vector.tensor_tensor(out=both[:, halves[h]], in0=sa[:, halves[h]], in1=sb[:, halves[h]], op=ALU.mult)
+            nc.vector.scalar_tensor_tensor(out=either[:, halves[h]], in0=both[:, halves[h]], scalar=1.0, in1=leak_sb[:, halves[h]], op0=ALU.subtract, op1=ALU.mult)
+        for h in range(2):
+            nc.vector.scalar_tensor_tensor(out=prod[:, halves[h]], in0=either[:, halves[h]], scalar=-1.5 / 0.7, in1=sr[:, halves[h]], op0=ALU.mult, op1=ALU.mult)
+            nc.vector.scalar_tensor_tensor(out=res[:, halves[h]], in0=cur_sb[:, halves[h]], scalar=neg_deg[:], in1=prod[:, halves[h]], op0=ALU.mult, op1=ALU.add)
+            nc.sync.dma_start(out=out[:, halves[h]], in_=res[:, halves[h]])

@@ -23,12 +23,19 @@ PASSES = K // K_PASS
 HALF = S // 2
 LIST_ROWS = 16
 FLOOR = 1e-18
+GENE_PIECES = ((0, 256), (256, 384), (384, 512))
+LOG_PIECES = 4
+LEAD = 64
+
+
+def entries(list_tile, cols):
+    return list_tile[:, cols.start // LIST_ROWS : cols.stop // LIST_ROWS]
 
 
 def tile_picked_ygrn_or_p_kernel(tc, x_words, x_scales, w1, leak, cur, deg, offs, act1, act2, rep1, out):
     nc = tc.nc
-    halves = [slice(h * HALF, (h + 1) * HALF) for h in range(2)]
-    list_halves = [slice(h * HALF // LIST_ROWS, (h + 1) * HALF // LIST_ROWS) for h in range(2)]
+    halves = [slice(0, HALF), slice(HALF, S)]
+    pieces = [slice(lo, hi) for lo, hi in GENE_PIECES]
 
     with ExitStack() as ctx:
         keep = ctx.enter_context(tc.tile_pool(name="keep", bufs=1))
@@ -48,17 +55,25 @@ def tile_picked_ygrn_or_p_kernel(tc, x_words, x_scales, w1, leak, cur, deg, offs
             nc.sync.dma_start(out=scales[32 * q : 32 * q + 4 * PASSES, :].bitcast(I32), in_=x_scales[:, 4 * q : 4 * q + 4, :].bitcast(I32))
 
         words = [keep.tile([P, T], I32, name="words%d" % g, align_bytes=64) for g in range(PASSES)]
-        w_raw = keep.tile([P, PASSES, PACK * M], F32, name="w_raw", align_bytes=64)
-        nc.sync.dma_start(out=words[0][:], in_=x_words[0].rearrange("p c t -> p (c t)").bitcast(I32))
-        nc.sync.dma_start(out=w_raw[:], in_=w1.rearrange("(g p j) m -> p g (j m)", g=PASSES, j=PACK))
-        nc.sync.dma_start(out=words[1][:], in_=x_words[1].rearrange("p c t -> p (c t)").bitcast(I32))
+        w_raw = [keep.tile([P, PACK, M], F32, name="w_raw%d" % g, align_bytes=64) for g in range(PASSES)]
 
-        lists = []
-        for name, src in (("act1_sb", act1), ("act2_sb", act2), ("rep1_sb", rep1)):
-            tile_ = keep.tile([P, U // LIST_ROWS], U16, name=name)
-            nc.sync.dma_start(tile_[:], src)
-            lists.append(tile_)
-        act1_sb, act2_sb, rep1_sb = lists
+        def load_words(g):
+            nc.sync.dma_start(out=words[g][:], in_=x_words[g].rearrange("p c t -> p (c t)").bitcast(I32))
+
+        def load_weights(g):
+            nc.sync.dma_start(out=w_raw[g][:], in_=w1[g * K_PASS : (g + 1) * K_PASS, :].rearrange("(p j) m -> p j m", j=PACK))
+
+        load_words(0)
+        load_weights(0)
+        load_weights(1)
+        load_words(1)
+
+        act1_sb = keep.tile([P, U // LIST_ROWS], U16, name="act1_sb")
+        act2_sb = keep.tile([P, U // LIST_ROWS], U16, name="act2_sb")
+        rep1_sb = keep.tile([P, U // LIST_ROWS], U16, name="rep1_sb")
+        nc.sync.dma_start(act1_sb[:], act1)
+        nc.sync.dma_start(act2_sb[:], act2)
+        nc.sync.dma_start(rep1_sb[:], rep1)
         leak_sb = keep.tile([P, U], F32, name="leak_sb")
         cur_sb = keep.tile([P, U], F32, name="cur_sb")
         deg_sb = keep.tile([P, 1], F32, name="deg_sb")
@@ -68,74 +83,85 @@ def tile_picked_ygrn_or_p_kernel(tc, x_words, x_scales, w1, leak, cur, deg, offs
         neg_deg = keep.tile([P, 1], F32, name="neg_deg")
         nc.gpsimd.tensor_scalar(out=neg_deg[:], in0=deg_sb[:], scalar1=-1.0, scalar2=0.0, op0=ALU.mult, op1=ALU.add)
 
+        picked = [keep.tile([P, S], U32, name="picked%d" % g, align_bytes=64) for g in range(PASSES)]
         picked_scales = keep.tile([P, S], U8, name="picked_scales", align_bytes=64)
-        nc.vector.tensor_copy(picked_scales[:], scales[:].indirect(offs_sb[:]))
-        picked, w_codes, w_scales = [], [], []
-        for g in range(PASSES):
-            picked_g = keep.tile([P, S], U32, name="picked%d" % g, align_bytes=64)
-            if g == 0:
-                nc.vector.tensor_copy(picked_g[:], words[g][:].bitcast(U32).indirect(offs_sb[:]))
-            picked.append(picked_g)
-            grouped = keep.tile([P, M, PACK], BF16, name="grouped%d" % g, align_bytes=64)
-            nc.scalar.copy(out=grouped[:], in_=w_raw[:, g, :].rearrange("p (j m) -> p m j", j=PACK))
-            codes = keep.tile([P, M], U32, name="w_codes%d" % g, align_bytes=64)
-            plane = keep.tile([P, M], U8, name="w_scales%d" % g, align_bytes=64)
-            nc.vector.quantize_mx(out=codes[:].bitcast(FP8X4), scales=plane[:], in_=grouped[:].rearrange("p m j -> p (m j)"))
-            w_codes.append(codes)
-            w_scales.append(plane)
+        w_codes = [keep.tile([P, M], U32, name="w_codes%d" % g, align_bytes=64) for g in range(PASSES)]
+        w_scales = [keep.tile([P, M], U8, name="w_scales%d" % g, align_bytes=64) for g in range(PASSES)]
+        grouped = [keep.tile([P, M, PACK], BF16, name="grouped%d" % g, align_bytes=64) for g in range(PASSES)]
 
-        for h in range(2):
-            nc.vector.tensor_copy(picked[1][:, halves[h]], words[1][:].bitcast(U32).indirect(offs_sb[:, list_halves[h]]))
-        banks = [psum.tile([P, HALF], F32, name="y%d" % h) for h in range(2)]
+        def quantize(g):
+            nc.scalar.copy(out=grouped[g][:], in_=w_raw[g][:].rearrange("p j m -> p m j"))
+            nc.vector.quantize_mx(out=w_codes[g][:].bitcast(FP8X4), scales=w_scales[g][:], in_=grouped[g][:].rearrange("p m j -> p (m j)"))
+
+        def pick(g, cols):
+            nc.vector.tensor_copy(picked[g][:, cols], words[g][:].bitcast(U32).indirect(entries(offs_sb, cols)))
+
+        def pick_scales():
+            nc.vector.tensor_copy(picked_scales[:], scales[:].indirect(offs_sb[:]))
+
+        pick(0, slice(0, S))
+        pick_scales()
+        quantize(0)
+        quantize(1)
+        for cols in pieces:
+            pick(1, cols)
+
+        banks = [psum.tile([P, c.stop - c.start], F32, name="y%d" % i) for i, c in enumerate(pieces)]
         for g in range(PASSES):
-            for h in range(2):
-                nc.tensor.matmul_mx(out=banks[h][:], lhsT=w_codes[g][:].bitcast(FP8X4), lhsT_scale=w_scales[g][:],
-                                    rhs=picked[g][:, halves[h]].bitcast(FP8X4), rhs_scale=picked_scales[4 * g :, halves[h]],
+            for bank, cols in zip(banks, pieces):
+                nc.tensor.matmul_mx(out=bank[:], lhsT=w_codes[g][:].bitcast(FP8X4), lhsT_scale=w_scales[g][:],
+                                    rhs=picked[g][:, cols].bitcast(FP8X4), rhs_scale=picked_scales[4 * g :, cols],
                                     start=(g == 0), stop=(g == PASSES - 1))
 
         sig = keep.tile([P, S], F32, name="sig")
         y_floor = keep.tile([P, S], F32, name="y_floor")
-        for h in range(2):
-            nc.scalar.activation(out=sig[:, halves[h]], in_=banks[h][:], func=ACT.Sigmoid, scale=-1.0)
-        for h in range(2):
-            nc.vector.tensor_scalar(out=y_floor[:, halves[h]], in0=banks[h][:], scalar1=FLOOR, scalar2=None, op0=ALU.max)
+        for bank, cols in zip(banks, pieces):
+            nc.scalar.activation(out=sig[:, cols], in_=bank[:], func=ACT.Sigmoid, scale=-1.0)
+        for bank, cols in zip(banks, pieces):
+            nc.vector.tensor_scalar(out=y_floor[:, cols], in0=bank[:], scalar1=FLOOR, scalar2=None, op0=ALU.max)
 
         neg_soft = keep.tile([P, S], F32, name="neg_soft")
         lev = keep.tile([P, S], F32, name="lev")
         log_lev = keep.tile([P, S], F32, name="log_lev")
 
         def part(t, i):
-            return t[:].rearrange("p (h c) -> p h c", h=2)[:, :, i * (HALF // 2) : (i + 1) * (HALF // 2)]
+            width = M // LOG_PIECES
+            return t[:].rearrange("p (h c) -> p h c", c=M)[:, :, i * width : (i + 1) * width]
 
-        for i in range(2):
+        for i in range(LOG_PIECES):
             nc.scalar.activation(out=part(neg_soft, i), in_=part(sig, i), func=ACT.Ln, bias=FLOOR)
             nc.vector.scalar_tensor_tensor(out=part(lev, i), in0=part(neg_soft, i), scalar=-1.0, in1=part(y_floor, i), op0=ALU.mult, op1=ALU.max)
-        for i in range(2):
+        for i in range(LOG_PIECES):
             nc.scalar.activation(out=part(log_lev, i), in_=part(lev, i), func=ACT.Ln)
 
-        LEAD = 64
-        logs = keep.tile([P, 2 * U + LEAD], F32, name="logs")
-        ua = [logs[:, 0:HALF], logs[:, U + LEAD + HALF :]]
-        ub = [logs[:, HALF:U], logs[:, U + LEAD : U + LEAD + HALF]]
-        sr = logs[:, U : 2 * U]
+        ua_tiles = [keep.tile([P, HALF], F32, name="ua%d" % h) for h in range(2)]
+        ua = [t[:] for t in ua_tiles]
+        ub0 = keep.tile([P, HALF], F32, name="ub0")
+        either1 = keep.tile([P, HALF], F32, name="either1")
+        shared = keep.tile([P, U], F32, name="shared")
+        ub = [ub0[:], shared[:, HALF // 2 : HALF // 2 + HALF]]
+        sr = [ua[1], shared[:, 0:HALF]]
+        either = [shared[:, HALF:U], either1[:]]
         sa = keep.tile([P, U], F32, name="sa")
         sb = keep.tile([P, U], F32, name="sb")
         both = keep.tile([P, U], F32, name="both")
-        either = keep.tile([P, U], F32, name="either")
         prod = keep.tile([P, U], F32, name="prod")
         res = keep.tile([P, U], F32, name="res")
         for h in range(2):
-            nc.vector.tensor_copy(ua[h], log_lev[:].indirect(act1_sb[:, list_halves[h]]))
-            nc.vector.tensor_copy(ub[h], log_lev[:].indirect(act2_sb[:, list_halves[h]]))
+            nc.vector.tensor_copy(ua[h], log_lev[:].indirect(entries(act1_sb, halves[h])))
+            nc.vector.tensor_copy(ub[h], log_lev[:].indirect(entries(act2_sb, halves[h])))
         for h in range(2):
             nc.scalar.activation(out=sa[:, halves[h]], in_=ua[h], func=ACT.Sigmoid, scale=-2.0, bias=math.log(0.5))
             nc.scalar.activation(out=sb[:, halves[h]], in_=ub[h], func=ACT.Sigmoid, scale=-2.0, bias=math.log(0.8))
-        for lo, hi in ((0, LEAD), (LEAD, HALF), (HALF, U)):
-            nc.scalar.activation(out=sr[:, lo:hi], in_=log_lev[:].indirect(rep1_sb[:, lo // LIST_ROWS : hi // LIST_ROWS]), func=ACT.Sigmoid, scale=-2.0, bias=math.log(0.7))
-        for h in range(2):
-            nc.vector.tensor_tensor(out=both[:, halves[h]], in0=sa[:, halves[h]], in1=sb[:, halves[h]], op=ALU.mult)
-            nc.vector.scalar_tensor_tensor(out=either[:, halves[h]], in0=both[:, halves[h]], scalar=1.0, in1=leak_sb[:, halves[h]], op0=ALU.subtract, op1=ALU.mult)
-        for h in range(2):
-            nc.vector.scalar_tensor_tensor(out=prod[:, halves[h]], in0=either[:, halves[h]], scalar=-1.5 / 0.7, in1=sr[:, halves[h]], op0=ALU.mult, op1=ALU.mult)
-            nc.vector.scalar_tensor_tensor(out=res[:, halves[h]], in0=cur_sb[:, halves[h]], scalar=neg_deg[:], in1=prod[:, halves[h]], op0=ALU.mult, op1=ALU.add)
-            nc.sync.dma_start(out=out[:, halves[h]], in_=res[:, halves[h]])
+        for dst, cols in ((sr[1][:, :LEAD], slice(HALF, HALF + LEAD)), (sr[0], halves[0]), (sr[1][:, LEAD:], slice(HALF + LEAD, U))):
+            nc.scalar.activation(out=dst, in_=log_lev[:].indirect(entries(rep1_sb, cols)), func=ACT.Sigmoid, scale=-2.0, bias=math.log(0.7))
+
+        for c in halves:
+            nc.vector.tensor_tensor(out=both[:, c], in0=sa[:, c], in1=sb[:, c], op=ALU.mult)
+        for h, c in enumerate(halves):
+            nc.vector.scalar_tensor_tensor(out=either[h], in0=both[:, c], scalar=1.0, in1=leak_sb[:, c], op0=ALU.subtract, op1=ALU.mult)
+        for h, c in enumerate(halves):
+            nc.vector.scalar_tensor_tensor(out=prod[:, c], in0=either[h], scalar=-1.5 / 0.7, in1=sr[h], op0=ALU.mult, op1=ALU.mult)
+        for c in halves:
+            nc.vector.scalar_tensor_tensor(out=res[:, c], in0=cur_sb[:, c], scalar=neg_deg[:], in1=prod[:, c], op0=ALU.mult, op1=ALU.add)
+            nc.sync.dma_start(out=out[:, c], in_=res[:, c])

@@ -41,11 +41,6 @@ def tile_picked_ygrn_or_p_kernel(tc, x_words, x_scales, w1, leak, cur, deg, offs
         keep = ctx.enter_context(tc.tile_pool(name="keep", bufs=1))
         psum = ctx.enter_context(tc.psum_pool(name="psum", bufs=1))
 
-        warm_in = keep.tile([P, 1], F32, name="warm_in")
-        warm_out = keep.tile([P, 1], F32, name="warm_out")
-        nc.gpsimd.memset(warm_in[:], 0.0)
-        nc.scalar.activation(out=warm_out[:], in_=warm_in[:], func=ACT.Sigmoid)
-
         offs_sb = keep.tile([P, S // LIST_ROWS], U16, name="offs_sb")
         nc.sync.dma_start(offs_sb[:], offs)
 
@@ -54,20 +49,28 @@ def tile_picked_ygrn_or_p_kernel(tc, x_words, x_scales, w1, leak, cur, deg, offs
         for q in range(4):
             nc.sync.dma_start(out=scales[32 * q : 32 * q + 4 * PASSES, :].bitcast(I32), in_=x_scales[:, 4 * q : 4 * q + 4, :].bitcast(I32))
 
+        warm_in = keep.tile([P, 1], F32, name="warm_in")
+        warm_out = keep.tile([P, 1], F32, name="warm_out")
+        nc.vector.memset(warm_in[:], 0.0)
+        nc.scalar.activation(out=warm_out[:], in_=warm_in[:], func=ACT.Sigmoid)
+
         words = [keep.tile([P, T], I32, name="words%d" % g, align_bytes=64) for g in range(PASSES)]
-        w_raw = [keep.tile([P, PACK, M], F32, name="w_raw%d" % g, align_bytes=64) for g in range(PASSES)]
+        w_raw = keep.tile([P, PASSES, PACK * M], F32, name="w_raw", align_bytes=64)
 
         def load_words(g):
             nc.sync.dma_start(out=words[g][:], in_=x_words[g].rearrange("p c t -> p (c t)").bitcast(I32))
 
-        def load_weights(g):
-            nc.sync.dma_start(out=w_raw[g][:], in_=w1[g * K_PASS : (g + 1) * K_PASS, :].rearrange("(p j) m -> p j m", j=PACK))
+        def load_weights():
+            nc.sync.dma_start(out=w_raw[:], in_=w1.rearrange("(g p j) m -> p g (j m)", g=PASSES, j=PACK))
 
         load_words(0)
-        load_weights(0)
-        load_weights(1)
+        load_weights()
         load_words(1)
 
+        cur_sb = keep.tile([P, U], F32, name="cur_sb")
+        deg_sb = keep.tile([P, 1], F32, name="deg_sb")
+        nc.sync.dma_start(out=deg_sb[:], in_=deg)
+        nc.sync.dma_start(out=cur_sb[:], in_=cur)
         act1_sb = keep.tile([P, U // LIST_ROWS], U16, name="act1_sb")
         act2_sb = keep.tile([P, U // LIST_ROWS], U16, name="act2_sb")
         rep1_sb = keep.tile([P, U // LIST_ROWS], U16, name="rep1_sb")
@@ -75,13 +78,7 @@ def tile_picked_ygrn_or_p_kernel(tc, x_words, x_scales, w1, leak, cur, deg, offs
         nc.sync.dma_start(act2_sb[:], act2)
         nc.sync.dma_start(rep1_sb[:], rep1)
         leak_sb = keep.tile([P, U], F32, name="leak_sb")
-        cur_sb = keep.tile([P, U], F32, name="cur_sb")
-        deg_sb = keep.tile([P, 1], F32, name="deg_sb")
-        nc.sync.dma_start(out=deg_sb[:], in_=deg)
         nc.sync.dma_start(out=leak_sb[:], in_=leak)
-        nc.sync.dma_start(out=cur_sb[:], in_=cur)
-        neg_deg = keep.tile([P, 1], F32, name="neg_deg")
-        nc.gpsimd.tensor_scalar(out=neg_deg[:], in0=deg_sb[:], scalar1=-1.0, scalar2=0.0, op0=ALU.mult, op1=ALU.add)
 
         picked = [keep.tile([P, S], U32, name="picked%d" % g, align_bytes=64) for g in range(PASSES)]
         picked_scales = keep.tile([P, S], U8, name="picked_scales", align_bytes=64)
@@ -90,7 +87,7 @@ def tile_picked_ygrn_or_p_kernel(tc, x_words, x_scales, w1, leak, cur, deg, offs
         grouped = [keep.tile([P, M, PACK], BF16, name="grouped%d" % g, align_bytes=64) for g in range(PASSES)]
 
         def quantize(g):
-            nc.scalar.copy(out=grouped[g][:], in_=w_raw[g][:].rearrange("p j m -> p m j"))
+            nc.scalar.copy(out=grouped[g][:], in_=w_raw[:, g, :].rearrange("p (j m) -> p m j", j=PACK))
             nc.vector.quantize_mx(out=w_codes[g][:].bitcast(FP8X4), scales=w_scales[g][:], in_=grouped[g][:].rearrange("p m j -> p (m j)"))
 
         def pick(g, cols):
@@ -102,8 +99,9 @@ def tile_picked_ygrn_or_p_kernel(tc, x_words, x_scales, w1, leak, cur, deg, offs
         pick(0, slice(0, S))
         pick_scales()
         quantize(0)
+        pick(1, pieces[0])
         quantize(1)
-        for cols in pieces:
+        for cols in pieces[1:]:
             pick(1, cols)
 
         banks = [psum.tile([P, c.stop - c.start], F32, name="y%d" % i) for i, c in enumerate(pieces)]
@@ -119,6 +117,9 @@ def tile_picked_ygrn_or_p_kernel(tc, x_words, x_scales, w1, leak, cur, deg, offs
             nc.scalar.activation(out=sig[:, cols], in_=bank[:], func=ACT.Sigmoid, scale=-1.0)
         for bank, cols in zip(banks, pieces):
             nc.vector.tensor_scalar(out=y_floor[:, cols], in0=bank[:], scalar1=FLOOR, scalar2=None, op0=ALU.max)
+
+        decay = keep.tile([P, U], F32, name="decay")
+        nc.vector.tensor_scalar(out=decay[:], in0=cur_sb[:], scalar1=deg_sb[:], scalar2=None, op0=ALU.mult)
 
         neg_soft = keep.tile([P, S], F32, name="neg_soft")
         lev = keep.tile([P, S], F32, name="lev")
@@ -163,5 +164,5 @@ def tile_picked_ygrn_or_p_kernel(tc, x_words, x_scales, w1, leak, cur, deg, offs
         for h, c in enumerate(halves):
             nc.vector.scalar_tensor_tensor(out=prod[:, c], in0=either[h], scalar=-1.5 / 0.7, in1=sr[h], op0=ALU.mult, op1=ALU.mult)
         for c in halves:
-            nc.vector.scalar_tensor_tensor(out=res[:, c], in0=cur_sb[:, c], scalar=neg_deg[:], in1=prod[:, c], op0=ALU.mult, op1=ALU.add)
+            nc.vector.tensor_tensor(out=res[:, c], in0=prod[:, c], in1=decay[:, c], op=ALU.subtract)
             nc.sync.dma_start(out=out[:, c], in_=res[:, c])

@@ -47,7 +47,7 @@ def tile_picked_ygrn_or_p_kernel(tc, x_words, x_scales, w1, leak, cur, deg, offs
         scales = keep.tile([P, T], U8, name="scales", align_bytes=64)
         nc.vector.memset(scales[:].bitcast(I32), 0)
         for q in range(4):
-            nc.sync.dma_start(out=scales[32 * q : 32 * q + 4 * PASSES, :].bitcast(I32), in_=x_scales[:, 4 * q : 4 * q + 4, :].bitcast(I32))
+            (nc.sync, nc.scalar)[q % 2].dma_start(out=scales[32 * q : 32 * q + 4 * PASSES, :].bitcast(I32), in_=x_scales[:, 4 * q : 4 * q + 4, :].bitcast(I32))
 
         warm_in = keep.tile([P, 1], F32, name="warm_in")
         warm_out = keep.tile([P, 1], F32, name="warm_out")

import math
from contextlib import ExitStack

import concourse.mybir as mybir

K, T, S, M, U = 1024, 1024, 512, 128, 512
FLOPS = 2 * K * M * S

F32 = mybir.dt.float32
BF16 = mybir.dt.bfloat16
I32 = mybir.dt.int32
U32 = mybir.dt.uint32
U16 = mybir.dt.uint16
U8 = mybir.dt.uint8
FP8X4 = mybir.dt.float8_e4m3fn_x4
ALU = mybir.AluOpType
ACT = mybir.ActivationFunctionType

P = 128
PACK = 4
K_PASS = P * PACK
PASSES = K // K_PASS
HALF = S // 2
LIST_ROWS = 16
FLOOR = 1e-18
GENE_PIECES = ((0, 256), (256, 384), (384, 512))
LOG_PIECES = 4
LEAD = 64


def entries(list_tile, cols):
    return list_tile[:, cols.start // LIST_ROWS : cols.stop // LIST_ROWS]


def tile_picked_ygrn_or_p_kernel(tc, x_words, x_scales, w1, leak, cur, deg, offs, act1, act2, rep1, out):
    nc = tc.nc
    halves = [slice(0, HALF), slice(HALF, S)]
    pieces = [slice(lo, hi) for lo, hi in GENE_PIECES]

    with ExitStack() as ctx:
        keep = ctx.enter_context(tc.tile_pool(name="keep", bufs=1))
        psum = ctx.enter_context(tc.psum_pool(name="psum", bufs=1))

        offs_sb = keep.tile([P, S // LIST_ROWS], U16, name="offs_sb")
        nc.sync.dma_start(offs_sb[:], offs)

        scales = keep.tile([P, T], U8, name="scales", align_bytes=64)
        nc.vector.memset(scales[:].bitcast(I32), 0)
        for q in range(4):
            (nc.sync, nc.scalar)[q % 2].dma_start(out=scales[32 * q : 32 * q + 4 * PASSES, :].bitcast(I32), in_=x_scales[:, 4 * q : 4 * q + 4, :].bitcast(I32))

        warm_in = keep.tile([P, 1], F32, name="warm_in")
        warm_out = keep.tile([P, 1], F32, name="warm_out")
        nc.vector.memset(warm_in[:], 0.0)
        nc.scalar.activation(out=warm_out[:], in_=warm_in[:], func=ACT.Sigmoid)

        words = [keep.tile([P, T], I32, name="words%d" % g, align_bytes=64) for g in range(PASSES)]
        w_raw = keep.tile([P, PASSES, PACK * M], F32, name="w_raw", align_bytes=64)

        def load_words(g):
            nc.sync.dma_start(out=words[g][:], in_=x_words[g].rearrange("p c t -> p (c t)").bitcast(I32))

        def load_weights():
            nc.sync.dma_start(out=w_raw[:], in_=w1.rearrange("(g p j) m -> p g (j m)", g=PASSES, j=PACK))

        load_words(0)
        load_weights()
        load_words(1)

        cur_sb = keep.tile([P, U], F32, name="cur_sb")
        deg_sb = keep.tile([P, 1], F32, name="deg_sb")
        nc.sync.dma_start(out=deg_sb[:], in_=deg)
        nc.sync.dma_start(out=cur_sb[:], in_=cur)
        act1_sb = keep.tile([P, U // LIST_ROWS], U16, name="act1_sb")
        act2_sb = keep.tile([P, U // LIST_ROWS], U16, name="act2_sb")
        rep1_sb = keep.tile([P, U // LIST_ROWS], U16, name="rep1_sb")
        nc.sync.dma_start(act1_sb[:], act1)
        nc.sync.dma_start(act2_sb[:], act2)
        nc.sync.dma_start(rep1_sb[:], rep1)
        leak_sb = keep.tile([P, U], F32, name="leak_sb")
        nc.sync.dma_start(out=leak_sb[:], in_=leak)

        picked = [keep.tile([P, S], U32, name="picked%d" % g, align_bytes=64) for g in range(PASSES)]
        picked_scales = keep.tile([P, S], U8, name="picked_scales", align_bytes=64)
        w_codes = [keep.tile([P, M], U32, name="w_codes%d" % g, align_bytes=64) for g in range(PASSES)]
        w_scales = [keep.tile([P, M], U8, name="w_scales%d" % g, align_bytes=64) for g in range(PASSES)]
        grouped = [keep.tile([P, M, PACK], BF16, name="grouped%d" % g, align_bytes=64) for g in range(PASSES)]

        def quantize(g):
            nc.scalar.copy(out=grouped[g][:], in_=w_raw[:, g, :].rearrange("p (j m) -> p m j", j=PACK))
            nc.vector.quantize_mx(out=w_codes[g][:].bitcast(FP8X4), scales=w_scales[g][:], in_=grouped[g][:].rearrange("p m j -> p (m j)"))

        def pick(g, cols):
            nc.vector.tensor_copy(picked[g][:, cols], words[g][:].bitcast(U32).indirect(entries(offs_sb, cols)))

        def pick_scales():
            nc.vector.tensor_copy(picked_scales[:], scales[:].indirect(offs_sb[:]))

        pick(0, slice(0, S))
        pick_scales()
        quantize(0)
        pick(1, pieces[0])
        quantize(1)
        for cols in pieces[1:]:
            pick(1, cols)

        banks = [psum.tile([P, c.stop - c.start], F32, name="y%d" % i) for i, c in enumerate(pieces)]
        for g in range(PASSES):
            for bank, cols in zip(banks, pieces):
                nc.tensor.matmul_mx(out=bank[:], lhsT=w_codes[g][:].bitcast(FP8X4), lhsT_scale=w_scales[g][:],
                                    rhs=picked[g][:, cols].bitcast(FP8X4), rhs_scale=picked_scales[4 * g :, cols],
                                    start=(g == 0), stop=(g == PASSES - 1))

        sig = keep.tile([P, S], F32, name="sig")
        y_floor = keep.tile([P, S], F32, name="y_floor")
        for bank, cols in zip(banks, pieces):
            nc.scalar.activation(out=sig[:, cols], in_=bank[:], func=ACT.Sigmoid, scale=-1.0)
        for bank, cols in zip(banks, pieces):
            nc.vector.tensor_scalar(out=y_floor[:, cols], in0=bank[:], scalar1=FLOOR, scalar2=None, op0=ALU.max)

        decay = keep.tile([P, U], F32, name="decay")
        nc.vector.tensor_scalar(out=decay[:], in0=cur_sb[:], scalar1=deg_sb[:], scalar2=None, op0=ALU.mult)

        neg_soft = keep.tile([P, S], F32, name="neg_soft")
        lev = keep.tile([P, S], F32, name="lev")
        log_lev = keep.tile([P, S], F32, name="log_lev")

        def part(t, i):
            width = M // LOG_PIECES
            return t[:].rearrange("p (h c) -> p h c", c=M)[:, :, i * width : (i + 1) * width]

        for i in range(LOG_PIECES):
            nc.scalar.activation(out=part(neg_soft, i), in_=part(sig, i), func=ACT.Ln, bias=FLOOR)
            nc.vector.scalar_tensor_tensor(out=part(lev, i), in0=part(neg_soft, i), scalar=-1.0, in1=part(y_floor, i), op0=ALU.mult, op1=ALU.max)
        for i in range(LOG_PIECES):
            nc.scalar.activation(out=part(log_lev, i), in_=part(lev, i), func=ACT.Ln)

        ua_tiles = [keep.tile([P, HALF], F32, name="ua%d" % h) for h in range(2)]
        ua = [t[:] for t in ua_tiles]
        ub0 = keep.tile([P, HALF], F32, name="ub0")
        either1 = keep.tile([P, HALF], F32, name="either1")
        shared = keep.tile([P, U], F32, name="shared")
        ub = [ub0[:], shared[:, HALF // 2 : HALF // 2 + HALF]]
        sr = [ua[1], shared[:, 0:HALF]]
        either = [shared[:, HALF:U], either1[:]]
        sa = keep.tile([P, U], F32, name="sa")
        sb = keep.tile([P, U], F32, name="sb")
        both = keep.tile([P, U], F32, name="both")
        prod = keep.tile([P, U], F32, name="prod")
        res = keep.tile([P, U], F32, name="res")
        for h in range(2):
            nc.vector.tensor_copy(ua[h], log_lev[:].indirect(entries(act1_sb, halves[h])))
            nc.vector.tensor_copy(ub[h], log_lev[:].indirect(entries(act2_sb, halves[h])))
        for h in range(2):
            nc.scalar.activation(out=sa[:, halves[h]], in_=ua[h], func=ACT.Sigmoid, scale=-2.0, bias=math.log(0.5))
            nc.scalar.activation(out=sb[:, halves[h]], in_=ub[h], func=ACT.Sigmoid, scale=-2.0, bias=math.log(0.8))
        for dst, cols in ((sr[1][:, :LEAD], slice(HALF, HALF + LEAD)), (sr[0], halves[0]), (sr[1][:, LEAD:], slice(HALF + LEAD, U))):
            nc.scalar.activation(out=dst, in_=log_lev[:].indirect(entries(rep1_sb, cols)), func=ACT.Sigmoid, scale=-2.0, bias=math.log(0.7))

        for c in halves:
            nc.vector.tensor_tensor(out=both[:, c], in0=sa[:, c], in1=sb[:, c], op=ALU.mult)
        for h, c in enumerate(halves):
            nc.vector.scalar_tensor_tensor(out=either[h], in0=both[:, c], scalar=1.0, in1=leak_sb[:, c], op0=ALU.subtract, op1=ALU.mult)
        for h, c in enumerate(halves):
            nc.vector.scalar_tensor_tensor(out=prod[:, c], in0=either[h], scalar=-1.5 / 0.7, in1=sr[h], op0=ALU.mult, op1=ALU.mult)
        for c in halves:
            nc.vector.tensor_tensor(out=res[:, c], in0=prod[:, c], in1=decay[:, c], op=ALU.subtract)
            nc.sync.dma_start(out=out[:, c], in_=res[:, c])
